import numpy as np, ml_dtypes
CORES = [21,109,149,237,277,365,405,493,150,406]
N = 10
TOK, K = 256, 3
ROUTE = [[[2,3,4],[1,2,4],[0,5,8],[1,3,9],[0,2,9],[2,3,7],[0,6,7],[1,6,8],[2,4,7],[1,7,9],[0,1,3],[1,3,6],[0,4,7],[1,3,8],[1,3,8],[3,6,7],[3,6,8],[4,5,8],[0,1,4],[1,2,7],[1,5,6],[6,7,9],[2,3,8],[0,2,6],[1,3,7],[2,7,8],[5,8,9],[4,5,8],[2,5,6],[1,7,9],[1,3,4],[0,8,9],[2,3,4],[0,7,9],[0,6,7],[0,7,9],[1,3,5],[3,4,7],[0,3,8],[1,7,9],[0,2,8],[1,6,8],[5,6,7],[1,6,9],[0,5,6],[7,8,9],[1,2,5],[4,7,9],[1,6,7],[2,8,9],[3,4,8],[1,7,9],[0,5,8],[0,4,7],[4,7,8],[0,3,4],[1,6,7],[0,1,3],[1,5,6],[0,6,9],[2,8,9],[7,8,9],[0,3,5],[0,1,2],[4,7,8],[2,5,8],[1,6,8],[0,3,9],[0,2,7],[3,5,9],[6,8,9],[0,4,7],[4,7,9],[2,3,8],[0,2,8],[0,3,4],[2,3,8],[1,8,9],[3,6,7],[0,3,9],[2,8,9],[0,3,7],[2,6,8],[1,4,7],[1,8,9],[2,3,9],[0,5,7],[0,1,6],[3,4,8],[4,5,8],[1,3,8],[0,6,8],[3,6,9],[3,5,6],[3,4,7],[1,5,6],[1,6,8],[1,6,7],[0,5,7],[2,4,8],[0,2,9],[2,4,9],[0,2,4],[0,5,6],[1,5,6],[0,2,3],[0,6,8],[5,8,9],[1,3,4],[0,1,9],[0,3,6],[0,1,6],[2,4,5],[2,4,5],[1,5,8],[1,2,4],[0,5,7],[4,8,9],[0,2,6],[0,3,5],[4,7,9],[1,5,8],[0,2,6],[4,5,7],[5,6,8],[0,1,5],[4,5,7],[0,3,8],[2,3,4],[2,3,7],[6,7,8],[6,8,9],[0,1,8],[1,3,4],[5,6,8],[0,2,5],[0,2,7],[1,2,6],[1,5,6],[3,5,6],[2,3,6],[1,5,7],[1,3,8],[0,4,7],[0,6,8],[0,3,7],[2,5,7],[2,4,6],[1,4,7],[1,3,5],[5,6,8],[2,4,8],[0,3,8],[1,3,8],[4,7,8],[0,4,9],[3,4,7],[4,6,7],[0,6,8],[0,2,3],[0,2,8],[1,5,7],[1,2,3],[3,6,9],[1,3,7],[0,2,6],[0,2,8],[0,4,5],[3,4,7],[3,5,6],[0,8,9],[3,6,7],[1,3,8],[3,8,9],[0,4,9],[1,4,7],[0,1,7],[2,8,9],[3,6,9],[1,6,8],[1,5,7],[3,4,6],[3,5,9],[4,5,9],[2,5,7],[0,1,5],[0,3,5],[0,5,9],[4,5,7],[3,4,7],[1,3,6],[2,5,8],[3,5,7],[3,4,9],[1,5,6],[5,6,7],[4,7,9],[1,3,5],[1,5,8],[1,6,8],[1,2,6],[0,3,8],[2,6,9],[1,4,8],[2,3,7],[5,6,9],[3,5,6],[0,6,9],[2,6,8],[1,5,9],[1,2,3],[1,5,7],[0,4,9],[4,5,7],[2,3,5],[3,6,9],[0,6,9],[5,6,9],[2,5,7],[0,1,3],[0,6,8],[1,2,9],[1,7,8],[1,2,5],[2,3,7],[0,4,5],[0,6,7],[3,4,6],[1,6,9],[1,3,8],[0,4,7],[1,2,3],[1,3,8],[0,4,6],[3,7,9],[4,6,8],[1,4,9],[0,3,5],[0,4,6],[2,8,9],[1,2,4],[1,3,5],[3,4,7],[1,3,9],[2,3,5],[1,2,5],[2,8,9],[2,4,5],[3,6,9],[0,3,6],[1,6,7],[3,4,6],[3,4,9],[0,5,9],[0,2,8],[1,4,8]],[[4,6,9],[0,1,3],[4,6,9],[2,6,8],[0,1,7],[1,2,5],[1,4,6],[3,4,9],[0,2,7],[0,7,9],[3,4,7],[1,7,9],[0,4,8],[5,6,9],[0,7,9],[0,3,9],[3,5,9],[3,5,7],[1,2,5],[2,6,8],[3,5,8],[5,8,9],[1,6,7],[3,5,6],[3,6,9],[0,2,9],[0,3,8],[1,3,5],[2,4,7],[2,5,9],[3,5,6],[0,1,8],[4,6,7],[6,7,9],[1,3,6],[3,5,8],[0,2,3],[0,3,6],[6,8,9],[2,5,7],[1,5,6],[5,6,9],[0,3,9],[1,4,8],[0,1,2],[1,6,9],[0,2,3],[1,2,7],[0,1,4],[0,3,8],[0,1,5],[0,6,7],[0,1,8],[4,5,9],[1,5,7],[5,8,9],[5,6,9],[1,2,8],[1,6,8],[2,3,9],[1,2,9],[4,7,8],[0,3,7],[4,7,9],[3,6,8],[3,6,7],[0,5,7],[3,5,7],[1,3,7],[1,7,9],[2,4,6],[2,6,7],[3,6,9],[2,3,5],[5,6,7],[4,5,9],[3,6,7],[1,5,7],[0,5,7],[2,3,8],[1,6,8],[2,3,4],[1,5,8],[6,8,9],[3,6,9],[5,7,9],[3,4,7],[0,4,8],[1,6,7],[2,4,5],[1,3,7],[2,6,8],[1,6,9],[1,3,8],[1,2,7],[3,4,6],[2,4,9],[2,5,7],[0,1,8],[5,6,9],[5,7,9],[0,5,6],[1,3,5],[2,3,4],[0,5,9],[2,4,9],[0,1,2],[3,4,6],[0,4,6],[1,3,5],[0,1,3],[1,2,4],[0,1,3],[1,4,7],[2,4,5],[0,6,8],[4,5,8],[0,5,9],[3,4,8],[3,8,9],[1,5,8],[4,7,9],[4,5,9],[4,6,7],[1,8,9],[2,5,8],[4,5,6],[1,5,7],[3,4,6],[0,8,9],[2,3,5],[0,2,5],[2,4,8],[4,5,9],[0,1,4],[1,3,9],[1,4,5],[2,6,9],[1,6,9],[1,3,8],[0,3,4],[2,5,7],[1,3,4],[0,5,7],[0,2,7],[0,1,8],[3,5,8],[0,1,7],[0,8,9],[1,4,5],[4,6,9],[0,1,2],[1,4,8],[0,6,7],[1,6,9],[4,5,6],[5,6,7],[2,3,4],[4,5,9],[0,1,2],[7,8,9],[2,7,8],[4,8,9],[2,6,8],[1,5,9],[2,3,4],[1,8,9],[1,4,9],[0,4,5],[1,2,9],[0,5,6],[0,4,9],[2,7,8],[0,5,6],[2,4,8],[0,1,3],[0,8,9],[1,4,5],[0,3,5],[1,3,8],[4,7,9],[1,5,8],[0,3,9],[0,8,9],[3,5,8],[1,2,5],[4,7,9],[5,6,9],[1,4,5],[2,6,7],[2,5,6],[3,4,6],[0,2,5],[3,4,7],[1,3,6],[0,1,3],[0,1,4],[2,3,7],[0,5,7],[2,7,8],[3,5,9],[2,5,8],[0,1,4],[0,1,6],[1,4,9],[2,3,7],[0,1,2],[0,4,7],[3,4,5],[0,4,9],[0,2,5],[0,1,5],[2,7,9],[2,3,5],[1,4,7],[1,4,6],[0,4,7],[4,7,9],[5,8,9],[1,4,6],[2,3,8],[3,7,8],[1,5,7],[1,6,8],[3,4,6],[4,5,6],[0,1,7],[0,4,6],[2,5,6],[2,5,8],[3,4,9],[0,4,7],[1,4,9],[2,3,5],[1,3,7],[1,2,6],[4,5,9],[1,4,8],[1,2,3],[0,3,8],[0,3,4],[0,4,6],[3,5,8],[0,6,8],[3,7,8],[6,7,9],[0,1,2],[0,3,6],[2,4,7],[1,7,8],[1,2,6],[2,3,9],[3,6,8],[0,2,7],[2,4,6],[1,2,5]],[[2,4,5],[1,2,3],[1,2,5],[0,8,9],[3,6,8],[1,2,6],[1,3,7],[1,3,6],[3,5,7],[1,5,8],[3,5,7],[1,6,9],[2,5,6],[1,3,9],[3,4,8],[2,7,9],[2,4,5],[0,3,7],[0,2,4],[2,5,7],[1,4,8],[2,4,9],[0,2,5],[0,3,7],[2,5,7],[1,4,8],[1,2,8],[2,4,5],[3,6,7],[3,8,9],[1,3,5],[5,8,9],[4,5,8],[3,5,7],[1,5,6],[0,5,6],[5,8,9],[0,4,5],[0,5,8],[1,5,7],[0,4,7],[1,4,7],[4,7,8],[0,1,5],[3,4,6],[1,3,8],[2,5,8],[0,6,8],[0,3,8],[3,5,8],[2,5,8],[2,4,6],[1,3,6],[0,3,7],[2,4,7],[2,3,4],[5,6,7],[2,4,5],[0,2,3],[0,2,4],[1,4,6],[0,5,9],[6,8,9],[2,3,9],[1,2,7],[0,2,7],[4,5,8],[2,3,7],[3,4,6],[2,3,9],[1,4,6],[2,3,7],[0,3,6],[4,5,7],[0,3,8],[1,5,7],[1,2,6],[0,8,9],[0,3,5],[1,4,9],[4,5,6],[4,5,6],[2,7,8],[0,7,9],[0,1,8],[2,6,9],[0,5,7],[1,3,8],[1,7,9],[0,1,7],[1,7,8],[1,8,9],[0,4,7],[1,7,8],[2,6,8],[1,4,5],[0,4,9],[2,5,9],[1,3,5],[2,4,8],[2,4,5],[2,5,9],[1,3,8],[3,6,8],[0,2,4],[0,7,9],[1,3,8],[1,2,5],[0,2,8],[4,7,8],[0,3,5],[2,3,4],[3,4,8],[0,5,8],[0,1,8],[1,3,7],[0,5,8],[1,2,6],[0,1,5],[3,7,8],[0,2,4],[1,6,7],[6,8,9],[0,7,9],[4,6,9],[2,6,7],[0,3,8],[5,6,7],[1,4,6],[1,4,9],[0,1,3],[2,3,9],[1,6,8],[1,4,9],[0,2,9],[1,2,9],[1,2,7],[3,4,9],[3,4,9],[1,2,6],[0,5,9],[1,4,7],[1,6,7],[2,7,8],[1,3,8],[3,4,6],[2,7,9],[0,5,8],[0,5,9],[1,4,7],[2,5,9],[2,4,5],[4,5,7],[3,4,8],[0,1,6],[2,5,6],[1,3,5],[1,5,6],[3,6,9],[0,3,4],[2,3,9],[0,6,9],[1,5,7],[1,6,9],[1,4,7],[2,3,8],[0,5,8],[1,4,8],[4,6,7],[0,7,9],[0,2,3],[0,4,5],[0,7,8],[2,7,8],[1,4,6],[3,4,8],[1,2,9],[4,6,9],[5,6,9],[0,4,8],[4,6,7],[7,8,9],[0,4,8],[0,4,5],[3,5,7],[4,8,9],[0,1,6],[2,7,8],[1,2,9],[2,3,4],[3,5,7],[1,3,4],[3,7,9],[0,2,4],[1,3,7],[1,6,9],[2,4,9],[0,3,9],[7,8,9],[4,7,9],[1,3,9],[2,3,6],[2,4,9],[0,4,8],[6,8,9],[1,6,9],[1,7,8],[0,3,4],[3,4,9],[4,6,9],[0,6,8],[6,8,9],[0,2,9],[1,6,7],[1,4,6],[0,2,8],[2,3,9],[1,3,5],[0,1,5],[1,2,7],[3,6,9],[0,5,9],[3,6,8],[0,2,7],[0,3,6],[1,2,7],[2,4,9],[2,4,5],[2,3,8],[4,7,8],[2,5,7],[0,5,6],[2,8,9],[0,3,6],[3,5,6],[2,3,6],[3,6,9],[0,7,8],[1,6,7],[4,6,8],[0,2,4],[5,8,9],[4,7,8],[0,3,4],[5,6,7],[2,3,4],[0,2,6],[2,4,5],[1,5,8],[4,5,8],[6,8,9],[2,5,6],[1,5,6],[3,6,8],[4,5,6],[0,5,7]],[[3,6,7],[1,2,5],[0,7,8],[0,4,6],[3,5,7],[4,6,9],[0,3,8],[1,2,8],[1,3,8],[0,2,9],[1,2,8],[1,4,5],[1,2,3],[1,4,6],[4,7,8],[0,2,6],[1,7,8],[0,4,6],[0,1,8],[0,3,8],[2,3,4],[0,2,9],[0,4,6],[3,6,8],[1,2,8],[1,5,6],[3,6,7],[1,2,8],[3,4,9],[2,4,9],[3,4,8],[0,1,8],[1,7,9],[1,3,7],[0,5,7],[0,1,2],[1,3,7],[2,6,8],[1,6,7],[1,3,7],[3,4,6],[4,8,9],[1,3,4],[0,6,8],[0,1,5],[1,4,8],[0,5,8],[0,2,7],[0,1,2],[0,1,6],[1,3,7],[0,7,9],[4,6,9],[2,3,5],[0,3,7],[1,4,9],[2,3,5],[0,6,8],[1,3,5],[0,4,7],[5,6,7],[1,5,9],[5,7,9],[2,5,8],[2,3,7],[0,2,9],[3,7,9],[5,6,7],[1,6,9],[2,4,8],[1,4,7],[1,4,8],[3,4,8],[3,5,8],[2,4,9],[2,6,9],[3,6,8],[1,5,9],[1,5,7],[1,2,4],[0,2,3],[0,6,7],[0,1,5],[2,6,7],[0,4,9],[2,5,6],[2,3,5],[1,7,8],[2,8,9],[5,6,9],[1,2,3],[3,4,9],[0,3,7],[4,5,9],[0,7,9],[2,4,6],[5,8,9],[0,5,7],[2,4,7],[2,5,8],[1,4,9],[3,7,9],[0,2,9],[1,2,8],[1,3,5],[0,4,9],[1,2,6],[2,7,9],[4,5,8],[1,6,8],[5,7,8],[1,3,6],[1,5,8],[3,5,8],[2,3,5],[1,2,6],[5,7,8],[2,7,8],[1,2,4],[0,7,8],[0,2,5],[3,4,6],[3,4,6],[4,5,8],[1,3,4],[2,6,7],[0,3,6],[3,4,9],[1,2,3],[1,3,8],[6,8,9],[4,7,8],[2,6,7],[1,4,9],[2,5,8],[0,7,8],[5,6,9],[1,6,8],[0,3,5],[2,3,8],[3,7,9],[4,5,9],[1,2,5],[1,4,6],[2,5,6],[0,3,5],[3,6,7],[0,5,6],[0,3,6],[5,6,7],[0,2,5],[3,4,9],[0,1,4],[4,7,9],[4,7,9],[4,5,8],[0,4,6],[1,2,6],[0,6,7],[2,7,9],[0,3,5],[6,8,9],[0,1,6],[3,5,6],[0,7,8],[6,7,8],[1,4,9],[0,8,9],[2,4,6],[1,6,9],[0,2,4],[0,5,9],[0,7,9],[3,8,9],[1,5,9],[4,6,8],[2,7,8],[1,7,9],[0,5,9],[4,6,7],[3,4,6],[1,4,5],[4,6,7],[3,5,7],[1,4,8],[1,7,9],[1,4,8],[6,8,9],[0,3,5],[0,1,5],[0,1,8],[1,7,9],[2,6,8],[1,2,9],[0,6,7],[5,8,9],[0,1,3],[2,3,7],[1,5,9],[6,7,8],[6,7,8],[1,7,8],[0,1,8],[1,3,5],[5,7,9],[4,8,9],[0,1,7],[5,6,8],[4,6,9],[6,7,8],[0,5,7],[0,5,7],[5,6,9],[2,3,4],[1,7,8],[0,1,6],[5,8,9],[1,3,4],[0,6,8],[0,6,8],[2,3,8],[3,4,5],[2,6,8],[0,3,8],[0,4,5],[2,4,7],[2,7,8],[4,8,9],[2,6,8],[0,1,4],[2,4,7],[3,6,8],[1,2,6],[1,4,5],[2,8,9],[2,4,5],[2,3,6],[1,3,6],[0,4,5],[0,1,2],[0,5,8],[0,4,5],[0,2,9],[2,3,7],[1,4,5],[0,2,8],[0,4,7],[6,7,8],[4,7,8],[5,7,9],[2,3,6],[5,6,8],[3,7,9],[1,3,5],[2,5,8],[3,5,9]],[[1,2,6],[3,4,8],[1,3,9],[2,5,9],[2,3,7],[1,6,9],[0,1,9],[2,3,4],[1,4,6],[5,6,8],[2,5,8],[6,7,8],[1,3,7],[0,2,8],[0,1,2],[0,4,9],[2,4,6],[1,4,5],[6,8,9],[2,3,7],[4,5,6],[0,2,5],[0,7,8],[0,1,6],[2,4,7],[0,1,2],[4,6,8],[4,6,7],[2,4,6],[1,5,6],[2,5,9],[1,6,8],[0,4,9],[0,3,7],[3,7,8],[1,3,9],[0,5,8],[2,4,9],[2,4,6],[0,2,8],[0,3,5],[0,7,8],[0,3,9],[2,5,8],[3,6,8],[1,4,8],[5,7,8],[1,2,4],[1,2,7],[1,4,5],[5,6,9],[1,6,8],[4,6,9],[3,4,6],[4,5,7],[0,8,9],[1,6,9],[1,4,9],[6,7,8],[0,6,9],[3,7,9],[1,6,8],[1,5,9],[1,7,8],[3,6,8],[1,4,8],[3,7,8],[3,5,7],[1,4,8],[2,5,9],[1,3,6],[0,4,5],[1,4,6],[2,3,8],[0,4,5],[0,3,6],[0,3,6],[0,7,9],[2,5,7],[0,1,7],[0,3,7],[0,5,9],[0,5,8],[0,5,7],[0,8,9],[2,5,6],[1,4,9],[0,1,4],[0,4,7],[0,1,8],[4,5,7],[0,1,2],[1,4,7],[0,2,3],[1,2,4],[3,6,7],[2,6,8],[1,3,4],[0,5,7],[1,2,7],[4,8,9],[0,4,6],[0,6,7],[0,1,5],[1,3,4],[1,2,7],[2,3,8],[1,2,8],[0,1,9],[1,2,6],[6,8,9],[2,7,9],[5,6,9],[2,6,7],[0,7,8],[5,6,8],[1,3,8],[0,7,9],[0,2,5],[1,8,9],[1,5,7],[4,6,8],[2,6,9],[0,1,7],[0,4,7],[2,8,9],[2,5,9],[2,7,9],[5,7,9],[3,6,9],[0,4,7],[0,5,9],[1,5,8],[2,6,9],[1,3,9],[1,7,9],[1,6,9],[2,5,8],[2,8,9],[0,1,7],[6,7,9],[2,8,9],[3,5,9],[3,4,8],[4,5,9],[1,2,9],[0,2,4],[2,6,9],[0,1,6],[3,4,7],[2,6,7],[4,7,9],[0,6,7],[1,2,7],[0,1,6],[1,2,4],[1,3,4],[6,7,9],[1,6,9],[0,2,5],[2,5,9],[1,2,8],[0,5,8],[1,4,7],[0,3,4],[0,7,9],[2,3,7],[1,4,6],[2,6,7],[0,6,7],[0,1,5],[0,1,3],[4,8,9],[1,8,9],[3,4,7],[3,7,9],[2,6,9],[2,6,7],[2,3,6],[3,5,8],[1,3,9],[4,6,9],[4,7,9],[3,4,8],[3,6,7],[5,8,9],[0,5,8],[3,6,9],[1,5,7],[1,4,5],[1,3,5],[0,8,9],[1,2,8],[5,7,9],[0,4,7],[0,6,9],[2,4,7],[0,5,7],[1,2,4],[1,5,9],[1,3,8],[0,3,4],[2,3,9],[1,3,6],[0,1,6],[1,6,8],[1,2,7],[4,6,8],[6,7,8],[0,1,7],[2,6,8],[1,4,5],[0,2,7],[2,4,9],[6,7,9],[1,2,6],[1,4,7],[4,5,7],[3,8,9],[2,7,8],[3,5,8],[0,2,8],[2,4,5],[2,3,5],[2,3,9],[1,2,9],[0,5,7],[2,6,9],[0,2,5],[2,8,9],[0,3,4],[1,7,8],[0,6,9],[2,6,9],[0,4,7],[1,2,8],[1,2,3],[1,3,5],[1,3,8],[0,6,9],[1,2,6],[0,1,9],[0,5,8],[1,4,9],[0,2,6],[4,7,9],[1,5,9],[2,4,7],[0,3,4],[0,5,7],[0,2,7],[0,5,7],[3,4,6],[5,8,9],[0,4,7],[1,6,9]],[[1,6,8],[0,2,6],[0,3,9],[5,7,9],[1,6,7],[1,3,4],[3,5,7],[5,7,8],[1,4,8],[2,5,8],[0,1,9],[2,8,9],[0,8,9],[0,1,7],[2,4,7],[2,5,8],[0,5,9],[0,4,8],[2,3,4],[4,7,9],[0,5,6],[1,2,3],[1,5,8],[1,6,8],[1,5,9],[0,1,6],[1,4,5],[1,7,8],[2,7,9],[6,7,9],[0,3,7],[0,2,8],[2,3,6],[2,3,5],[0,2,3],[2,7,8],[0,4,9],[2,4,9],[3,4,5],[0,1,4],[7,8,9],[2,4,7],[4,5,7],[2,5,7],[3,7,8],[0,6,8],[2,4,5],[2,5,9],[1,2,7],[2,4,7],[5,8,9],[2,5,9],[0,1,6],[0,1,2],[1,2,9],[2,3,7],[0,1,3],[6,7,8],[1,4,9],[0,2,6],[1,5,6],[0,3,6],[3,7,9],[2,3,9],[3,4,5],[0,8,9],[1,4,8],[0,2,3],[1,7,9],[2,3,5],[1,8,9],[0,4,9],[5,6,7],[0,2,8],[3,4,6],[2,4,9],[4,5,8],[3,6,7],[0,1,6],[1,2,5],[1,8,9],[1,3,6],[0,2,9],[1,4,5],[0,8,9],[1,4,7],[1,5,7],[1,4,7],[0,3,7],[5,7,9],[2,8,9],[5,6,9],[5,6,7],[4,5,9],[3,4,7],[2,6,7],[2,6,7],[0,7,9],[1,5,6],[1,5,7],[0,1,5],[0,7,8],[3,4,9],[0,3,5],[2,3,5],[0,2,4],[0,4,6],[1,4,6],[4,8,9],[0,3,8],[4,5,6],[3,4,7],[2,4,9],[1,6,9],[3,7,8],[3,5,8],[2,6,9],[0,6,7],[1,6,8],[0,1,2],[2,5,9],[2,5,7],[2,4,8],[1,2,5],[0,2,3],[4,5,9],[2,4,9],[1,2,9],[5,6,9],[0,1,4],[0,1,2],[4,8,9],[2,5,7],[0,5,8],[0,5,8],[1,5,6],[0,2,5],[5,6,7],[3,4,8],[3,4,9],[3,4,9],[2,4,6],[2,3,4],[3,5,9],[6,8,9],[0,3,4],[6,7,9],[3,5,7],[0,1,3],[4,5,9],[3,6,8],[1,6,7],[1,2,3],[2,5,9],[3,5,9],[0,4,5],[4,7,8],[1,2,9],[1,3,8],[7,8,9],[3,5,7],[0,4,8],[0,8,9],[0,4,8],[7,8,9],[0,4,9],[3,7,9],[1,7,9],[1,4,8],[4,6,7],[0,2,6],[1,3,9],[0,3,7],[3,7,8],[0,3,7],[4,7,8],[1,4,7],[0,2,7],[1,6,7],[5,7,9],[1,2,6],[0,5,6],[3,4,7],[2,7,9],[2,4,7],[0,2,6],[0,4,6],[1,4,7],[0,4,6],[4,5,7],[0,8,9],[3,7,8],[2,3,6],[2,4,6],[2,3,9],[4,5,9],[1,7,9],[2,4,8],[3,4,8],[1,6,7],[0,1,4],[0,1,9],[0,1,6],[0,3,4],[0,1,4],[2,3,6],[1,3,4],[1,4,6],[0,1,6],[2,6,9],[1,3,8],[0,7,8],[2,3,9],[2,5,6],[2,6,9],[4,6,9],[4,5,6],[4,5,9],[2,3,7],[1,2,7],[3,5,8],[0,1,3],[1,3,9],[1,5,6],[3,4,9],[3,5,8],[3,5,7],[4,5,7],[0,2,7],[4,5,6],[1,3,4],[0,2,8],[4,6,9],[1,6,8],[1,5,6],[1,7,9],[1,3,6],[1,2,6],[3,4,9],[5,6,7],[4,6,8],[6,7,9],[1,2,6],[1,3,4],[3,7,9],[0,2,9],[0,1,4],[3,5,9],[0,3,4],[0,5,9],[0,4,7],[7,8,9],[2,6,8],[1,3,4],[3,5,6],[2,4,6]],[[1,5,6],[2,4,9],[0,4,7],[3,4,8],[1,7,9],[3,6,7],[1,6,8],[2,4,8],[1,5,8],[1,3,9],[0,4,5],[3,5,9],[6,7,9],[0,3,9],[0,2,4],[4,5,6],[2,5,9],[5,6,8],[0,3,6],[2,5,8],[1,3,4],[4,5,6],[0,2,9],[3,4,5],[1,3,8],[0,4,5],[1,4,5],[0,2,4],[3,4,9],[0,1,3],[3,5,9],[0,5,8],[0,5,7],[1,6,7],[2,8,9],[1,3,6],[3,4,9],[0,6,9],[0,2,5],[2,6,9],[7,8,9],[0,1,6],[1,7,8],[0,4,6],[5,6,8],[4,6,9],[5,6,9],[3,4,5],[0,2,9],[2,8,9],[5,8,9],[3,5,6],[6,7,8],[4,5,8],[1,2,7],[1,2,4],[2,4,7],[2,4,5],[1,3,8],[0,6,8],[0,5,7],[1,7,8],[5,8,9],[7,8,9],[2,3,4],[6,8,9],[0,4,8],[2,7,8],[1,5,8],[1,3,9],[1,5,8],[0,3,7],[4,6,8],[5,6,7],[0,4,7],[0,5,6],[3,4,5],[0,4,7],[0,3,8],[0,2,3],[1,6,7],[2,6,8],[1,6,7],[0,5,6],[1,3,7],[2,8,9],[0,2,6],[0,2,6],[1,2,4],[1,3,6],[1,3,8],[2,4,5],[0,5,6],[0,1,3],[0,5,8],[6,7,8],[6,8,9],[3,5,8],[0,1,7],[1,2,4],[5,8,9],[1,4,5],[0,2,9],[3,4,6],[3,4,5],[3,5,9],[0,2,5],[3,5,6],[1,6,7],[0,1,5],[2,6,8],[2,6,9],[0,2,6],[0,1,5],[3,6,9],[2,3,9],[2,4,7],[1,6,7],[1,2,6],[7,8,9],[6,7,9],[0,6,8],[2,5,7],[1,3,9],[0,7,9],[1,2,8],[5,7,8],[0,2,9],[0,4,5],[2,6,9],[2,7,9],[1,6,8],[4,7,8],[5,7,9],[6,7,8],[6,8,9],[1,3,6],[5,7,9],[1,3,9],[0,1,3],[0,2,7],[5,8,9],[4,5,8],[2,4,6],[1,3,5],[3,4,9],[1,4,8],[3,6,9],[0,2,3],[1,3,7],[0,2,5],[0,5,7],[2,6,9],[6,7,9],[1,3,5],[5,7,9],[0,1,3],[3,4,6],[0,4,9],[1,5,7],[2,4,7],[2,4,5],[2,3,4],[1,2,9],[1,2,7],[2,3,7],[0,6,7],[0,3,9],[4,8,9],[3,4,6],[0,7,9],[0,5,9],[5,7,9],[0,7,8],[0,1,2],[1,3,5],[3,5,9],[1,6,7],[1,3,4],[0,3,9],[4,5,9],[1,2,3],[6,7,8],[1,7,9],[3,4,9],[2,3,6],[0,5,8],[2,7,8],[0,1,8],[0,5,7],[1,4,7],[0,5,8],[2,5,7],[4,5,8],[0,1,6],[1,5,7],[0,6,8],[0,4,8],[3,6,8],[0,4,6],[3,4,8],[2,3,9],[3,7,9],[0,3,7],[6,8,9],[3,6,8],[0,1,2],[5,6,9],[1,2,7],[0,1,8],[2,3,8],[1,2,3],[0,1,4],[1,5,8],[0,4,7],[2,3,6],[6,8,9],[2,3,7],[0,2,8],[0,2,3],[0,2,6],[3,5,6],[0,6,9],[0,4,8],[1,3,8],[2,3,9],[2,6,7],[1,2,6],[2,4,9],[2,4,8],[1,5,7],[3,6,9],[0,4,9],[0,1,2],[1,3,7],[3,6,8],[3,7,8],[2,4,9],[0,3,8],[1,7,9],[1,7,8],[3,6,7],[2,6,9],[0,4,9],[4,5,7],[7,8,9],[2,4,5],[3,4,7],[2,8,9],[0,6,7],[2,5,6],[5,7,9],[2,4,9],[0,1,6],[1,3,6],[3,6,7]],[[1,2,4],[0,1,5],[5,7,8],[3,4,9],[3,4,9],[4,6,9],[1,3,7],[0,2,9],[2,4,8],[1,2,7],[0,4,6],[2,6,9],[2,4,9],[2,3,4],[1,3,5],[2,4,6],[3,4,9],[4,5,6],[2,6,8],[0,2,9],[0,8,9],[6,8,9],[1,2,3],[3,7,8],[0,5,7],[3,5,8],[4,5,8],[4,7,8],[1,2,8],[1,3,4],[1,3,4],[5,6,8],[2,5,9],[3,6,8],[1,5,8],[1,5,9],[2,7,8],[0,6,9],[2,4,6],[0,7,9],[3,7,9],[1,7,9],[1,7,8],[4,6,8],[1,4,7],[6,7,9],[3,4,5],[5,6,9],[0,4,6],[4,6,7],[1,6,8],[1,3,5],[7,8,9],[1,7,8],[0,3,4],[5,6,9],[5,6,7],[5,7,8],[2,6,7],[7,8,9],[1,5,7],[0,2,4],[1,2,7],[7,8,9],[2,3,4],[2,7,9],[5,6,8],[3,4,5],[5,6,8],[5,7,9],[3,8,9],[1,2,5],[2,3,7],[2,3,9],[2,7,9],[1,4,7],[0,3,9],[0,6,9],[3,5,7],[0,3,9],[2,3,8],[3,7,9],[0,7,8],[1,3,8],[2,5,9],[1,3,8],[1,7,9],[5,7,8],[1,3,4],[3,5,9],[2,5,6],[0,5,7],[2,4,9],[7,8,9],[1,4,5],[2,3,4],[0,5,6],[2,6,7],[3,4,8],[4,7,9],[0,2,8],[3,5,7],[3,7,9],[3,7,9],[2,4,8],[2,6,9],[1,4,8],[1,2,4],[5,6,9],[2,4,6],[0,3,7],[3,4,6],[2,5,6],[0,1,4],[4,5,6],[1,3,6],[0,3,7],[7,8,9],[1,2,6],[2,4,5],[0,7,8],[3,4,7],[0,1,6],[0,5,6],[1,2,5],[0,1,4],[3,6,9],[0,1,9],[2,8,9],[6,7,8],[1,3,8],[1,4,5],[1,2,3],[0,4,9],[0,3,7],[1,2,4],[1,5,8],[3,4,8],[0,7,9],[1,3,4],[1,3,6],[2,7,9],[2,7,9],[2,3,5],[3,4,7],[1,2,4],[5,6,8],[5,6,7],[5,6,8],[1,3,6],[2,7,9],[7,8,9],[4,6,9],[1,4,7],[1,8,9],[0,1,3],[2,3,7],[5,6,7],[4,5,9],[3,5,8],[0,1,2],[6,8,9],[0,3,5],[2,4,8],[0,2,6],[1,2,4],[1,5,9],[5,6,9],[5,6,7],[1,2,6],[3,4,8],[2,7,9],[0,3,6],[0,1,7],[2,3,9],[1,2,7],[2,4,8],[0,6,8],[0,2,3],[1,3,4],[0,1,5],[6,8,9],[0,8,9],[1,8,9],[0,3,8],[1,7,9],[1,7,9],[1,3,6],[0,4,9],[1,6,8],[0,5,7],[1,3,5],[1,6,8],[5,7,9],[1,3,4],[1,5,7],[0,1,2],[3,7,9],[2,6,8],[1,2,8],[3,4,6],[2,5,9],[1,3,7],[0,3,4],[2,3,7],[1,2,3],[0,5,8],[2,3,7],[0,5,8],[0,3,6],[3,5,8],[0,4,7],[0,3,6],[2,6,7],[0,5,9],[6,8,9],[6,8,9],[1,3,8],[2,3,6],[2,6,7],[3,4,7],[2,3,6],[2,5,7],[5,7,8],[0,1,9],[0,1,5],[0,3,4],[0,4,7],[2,4,9],[5,7,8],[3,4,7],[2,6,7],[1,6,9],[0,7,9],[0,5,6],[1,2,5],[2,7,9],[2,3,4],[1,8,9],[2,4,9],[0,2,8],[2,6,9],[5,7,9],[0,5,6],[4,5,6],[0,7,8],[2,7,9],[2,3,7],[1,7,9],[4,6,7],[7,8,9],[0,4,6],[0,2,3],[0,4,6],[0,2,3],[2,3,8]],[[1,3,6],[0,1,4],[0,1,8],[4,5,7],[0,6,9],[1,3,9],[7,8,9],[4,6,7],[0,4,8],[1,5,8],[0,6,7],[0,7,9],[0,2,8],[0,1,5],[2,3,4],[0,1,4],[0,6,9],[2,3,7],[1,7,9],[0,1,9],[1,5,6],[3,5,9],[0,5,6],[3,5,7],[3,4,6],[2,7,9],[0,4,5],[0,5,8],[0,2,7],[3,5,8],[2,6,9],[1,2,8],[2,5,6],[2,7,8],[0,1,3],[1,3,9],[5,8,9],[4,5,7],[2,4,6],[0,7,9],[2,5,9],[1,3,9],[4,7,9],[0,2,6],[3,6,9],[1,3,8],[2,3,4],[0,3,9],[1,6,9],[1,2,6],[1,2,9],[4,7,8],[0,4,7],[0,1,4],[0,4,5],[4,8,9],[0,5,8],[1,7,9],[3,4,6],[3,4,7],[2,3,7],[2,7,9],[0,3,9],[4,5,8],[1,3,9],[4,7,9],[1,7,8],[1,6,7],[1,3,6],[3,4,5],[3,6,7],[0,2,9],[1,7,8],[2,7,8],[0,4,9],[3,6,7],[3,4,6],[2,3,7],[1,5,7],[1,4,5],[0,1,7],[0,3,5],[3,5,9],[2,5,7],[0,6,9],[5,7,9],[4,7,9],[1,4,8],[4,7,8],[3,4,6],[2,4,5],[2,3,6],[1,4,9],[0,3,7],[0,1,7],[0,3,4],[3,8,9],[1,7,8],[0,7,8],[1,2,7],[1,2,5],[3,7,8],[0,3,8],[1,6,7],[1,5,6],[2,3,4],[5,6,7],[3,4,7],[0,4,7],[1,8,9],[1,2,7],[1,5,8],[0,7,8],[3,5,7],[1,2,4],[6,7,8],[1,6,8],[4,7,9],[1,7,8],[2,3,5],[0,8,9],[0,2,3],[0,2,7],[3,6,8],[1,6,7],[0,3,5],[2,5,6],[4,5,6],[6,8,9],[2,8,9],[1,3,4],[0,3,4],[1,6,9],[0,2,9],[1,2,5],[4,5,8],[0,6,8],[0,3,8],[0,4,8],[1,7,9],[0,2,9],[2,5,8],[1,2,5],[3,7,9],[0,5,6],[1,5,7],[3,4,6],[2,3,8],[1,6,9],[4,6,9],[0,5,6],[3,4,5],[0,4,8],[4,5,6],[1,3,8],[2,5,8],[0,6,8],[3,7,8],[2,6,8],[0,1,7],[3,5,6],[2,6,9],[3,5,9],[1,2,9],[1,7,8],[5,7,9],[5,6,8],[0,2,6],[4,5,6],[4,7,9],[0,2,8],[0,1,3],[2,3,9],[1,2,6],[0,2,9],[4,5,7],[4,8,9],[0,1,8],[1,3,8],[2,3,9],[4,8,9],[2,7,9],[4,5,6],[0,7,9],[0,3,4],[0,2,3],[2,5,9],[0,1,5],[2,6,8],[2,3,5],[2,3,6],[0,5,6],[2,6,8],[0,3,5],[4,8,9],[1,7,9],[1,6,8],[2,3,7],[4,5,7],[1,4,9],[2,4,7],[1,6,7],[1,4,6],[0,2,7],[1,3,4],[1,2,4],[1,5,7],[0,4,7],[0,4,7],[0,5,8],[4,5,8],[2,8,9],[1,4,9],[1,4,6],[1,2,8],[2,3,7],[3,5,7],[2,6,9],[3,7,8],[2,6,7],[1,5,9],[2,3,5],[2,3,7],[2,5,7],[5,6,9],[3,4,5],[5,8,9],[1,3,4],[2,4,6],[2,4,7],[0,2,8],[4,5,7],[0,5,7],[2,3,6],[4,5,6],[1,7,8],[2,3,7],[3,6,7],[0,6,8],[2,5,6],[3,5,6],[4,6,9],[0,1,7],[2,5,7],[1,2,6],[1,4,5],[0,6,9],[0,1,4],[1,4,8],[1,2,7],[2,4,6],[4,6,7],[2,6,9],[5,7,9],[0,3,7],[0,1,8]],[[3,4,7],[2,6,7],[5,6,8],[2,6,7],[0,5,8],[7,8,9],[1,3,5],[0,3,5],[2,3,5],[2,4,6],[1,6,8],[4,6,7],[3,6,9],[0,5,8],[0,6,8],[4,6,9],[1,2,7],[1,4,9],[0,3,5],[1,8,9],[2,3,9],[2,7,8],[3,4,7],[3,4,8],[0,4,5],[4,5,7],[2,3,4],[6,7,8],[0,5,9],[1,2,6],[0,5,8],[2,5,6],[2,7,9],[0,4,9],[1,5,7],[3,4,7],[0,2,3],[0,2,6],[0,2,9],[1,5,6],[1,4,8],[5,7,9],[4,5,9],[3,7,9],[0,4,9],[4,5,7],[2,5,7],[0,5,7],[4,5,6],[2,6,8],[1,5,9],[2,4,9],[0,2,4],[3,4,7],[1,3,8],[1,5,6],[0,1,9],[1,6,8],[4,5,6],[0,7,8],[2,5,9],[2,4,6],[2,4,8],[2,8,9],[1,2,4],[2,5,9],[0,1,3],[0,4,5],[2,3,8],[2,3,5],[4,5,6],[0,5,7],[1,4,8],[0,6,7],[2,7,8],[1,4,5],[1,3,4],[5,7,9],[1,2,3],[0,3,9],[0,2,5],[2,3,5],[4,6,8],[2,3,4],[0,7,9],[2,3,9],[3,6,7],[1,6,7],[2,4,5],[1,3,9],[0,6,9],[4,7,8],[4,6,9],[1,3,4],[0,1,9],[3,4,8],[0,3,9],[4,6,9],[2,3,8],[0,4,5],[1,5,9],[1,2,4],[7,8,9],[1,5,7],[1,6,9],[1,2,6],[1,4,9],[2,3,7],[1,6,9],[0,2,6],[4,5,8],[2,5,6],[3,5,8],[4,5,6],[1,3,4],[0,2,9],[2,5,6],[1,2,4],[1,2,6],[0,3,8],[0,5,6],[4,5,9],[1,2,4],[0,1,8],[0,3,6],[4,6,8],[4,5,9],[0,3,4],[5,7,9],[3,4,5],[2,4,8],[3,6,7],[2,6,9],[4,7,8],[1,7,9],[1,2,7],[3,4,9],[7,8,9],[4,7,8],[1,3,6],[1,3,7],[7,8,9],[5,6,8],[0,1,8],[1,3,5],[2,5,7],[1,2,9],[2,3,5],[3,6,7],[0,1,7],[0,3,5],[2,3,7],[0,2,3],[0,4,6],[0,5,7],[0,1,3],[0,3,4],[1,5,6],[0,3,9],[0,3,5],[3,7,8],[1,6,8],[2,3,7],[0,4,7],[0,4,6],[0,3,4],[0,4,6],[4,6,9],[1,3,6],[2,5,8],[0,2,8],[4,8,9],[0,2,4],[0,1,2],[0,2,9],[0,2,9],[2,4,6],[7,8,9],[0,1,7],[0,3,4],[2,6,9],[2,6,9],[2,5,8],[1,2,3],[3,4,7],[3,5,8],[1,3,9],[1,4,8],[2,6,7],[1,6,9],[3,4,9],[0,3,9],[0,3,7],[0,2,7],[0,5,9],[2,6,7],[0,3,7],[4,6,9],[2,4,9],[0,1,7],[1,5,7],[0,4,6],[1,2,7],[6,7,8],[3,5,7],[0,3,7],[2,3,5],[4,6,8],[1,5,9],[4,6,9],[0,1,3],[5,7,9],[3,5,7],[6,7,8],[1,8,9],[5,8,9],[1,4,9],[0,1,9],[1,4,6],[0,2,6],[1,4,7],[6,7,9],[0,5,7],[0,3,9],[0,5,8],[3,4,5],[1,5,8],[4,8,9],[5,7,9],[0,1,8],[0,7,9],[4,5,7],[1,3,6],[1,2,5],[0,2,6],[0,1,6],[0,6,7],[0,3,6],[0,4,9],[1,4,7],[2,6,9],[0,2,8],[4,5,8],[4,6,9],[1,7,9],[4,5,6],[4,6,7],[0,1,6],[0,4,8],[1,5,7],[2,6,9],[1,3,4],[0,7,9],[0,4,5],[3,5,9],[1,2,8]]]
def setup_inputs(rng):
    rt = (0.75 * rng.standard_normal((128, 1), dtype=np.float32) + rng.standard_normal((128, N), dtype=np.float32) / 2).astype(ml_dtypes.bfloat16)
    rm = np.zeros((N, N, TOK), np.float32)
    for r in range(N):
        for t in range(TOK): rm[r, ROUTE[r][t], t] = 1.0
    return {"x": rng.standard_normal((N, 128, TOK), dtype=np.float32).astype(ml_dtypes.bfloat16), "rt": np.broadcast_to(rt, (N, 128, N)).copy(), "rm": rm.astype(ml_dtypes.bfloat16), "w": rng.standard_normal((N, 128, 128), dtype=np.float32).astype(ml_dtypes.bfloat16)}
def setup_inputs_big(rng):
    d = setup_inputs(rng)
    for k in ("x", "w"): d[k] = (d[k].astype(np.float32) * 1024.0).astype(d[k].dtype)
    return d
def setup_inputs_small(rng):
    d = setup_inputs(rng)
    for k in ("x", "w"): d[k] = (d[k].astype(np.float32) * (1 / 1024.0)).astype(d[k].dtype)
    return d
def setup_inputs_apart(rng):
    d = setup_inputs(rng)
    f = (10.0 ** rng.permutation(np.linspace(-1.5, 1.5, N))).astype(np.float32).reshape(N, 1, 1)
    for k in ("x",): d[k] = (d[k].astype(np.float32) * f).astype(d[k].dtype)
    return d
def setup_inputs_lure(rng):
    d = setup_inputs(rng); x = d["x"].astype(np.float32) * 1024; rt = d["rt"][0].astype(np.float32)
    for r in range(N):
        for t in range(TOK):
            u = int(rng.choice([e for e in range(N) if e not in ROUTE[r][t]]))
            x[r][:, t] += 2097152 * (rt[:, u] - rt[:, ROUTE[r][t][0]])
    d["x"] = x.astype(d["x"].dtype)
    return d
def reference(x, rt, rm, w):
    X, RT, W = x.astype(np.float64), rt.astype(np.float64), w.astype(np.float64)
    y = np.zeros((N, 128, TOK))
    for r in range(N):
        sc = RT[r].T @ X[r]
        for t in range(TOK):
            ex = ROUTE[r][t]; g = np.exp(sc[ex, t] - sc[ex, t].max()); g = g / g.sum()
            y[r][:, t] = sum(g[i] * (W[e].T @ X[r][:, t]) for i, e in enumerate(ex))
    return {"y": y.astype(ml_dtypes.bfloat16)}

@@ -1,0 +1,230 @@
+from concourse.bass import DstId, RemoteDMATransfer
+from concourse.mybir import AluOpType, AxisListType, ActivationFunctionType
+
+NSIM = 512
+N, TOK, D = 10, 256, 128
+BIG = 1e29
+NB = 4
+
+SCRATCH = {
+    "wd": ("dram", [128, 128], "bfloat16"),
+    "wall": ("sbuf", [128, N * D], "bfloat16"),
+    "xs": ("sbuf", [128, TOK], "bfloat16"),
+    "rts": ("sbuf", [128, N], "bfloat16"),
+    "rms": ("sbuf", [128, TOK], "bfloat16"),
+    "ones": ("sbuf", [128, 128], "bfloat16"),
+    "ident": ("sbuf", [128, 128], "bfloat16"),
+    "sel": ("sbuf", [128, N * D], "bfloat16"),
+    "pen": ("sbuf", [128, 2 * N], "float32"),
+    "msk": ("sbuf", [128, 2 * N], "float32"),
+    "negm": ("sbuf", [128, 2], "float32"),
+    "ex": ("sbuf", [128, 2 * N], "float32"),
+    "ssum": ("sbuf", [128, 2], "float32"),
+    "rs": ("sbuf", [128, 2], "float32"),
+    "gt": ("sbuf", [128, 2 * N], "bfloat16"),
+    "g10": ("sbuf", [128, TOK], "bfloat16"),
+    "xg": ("sbuf", [128, N * TOK], "bfloat16"),
+    "ys": ("sbuf", [128, TOK], "bfloat16"),
+    "ps_s": ("psum", [128, 512], "float32"),
+    "ps_m": ("psum", [128, 512], "float32"),
+    "ps_g": ("psum", [128, 512], "float32"),
+    "ps_y": ("psum", [128, 512], "float32"),
+    "ps_b0": ("psum", [128, 512], "float32"),
+    "ps_b1": ("psum", [128, 512], "float32"),
+    "ps_b2": ("psum", [128, 512], "float32"),
+    "ps_b3": ("psum", [128, 512], "float32"),
+}
+SEMAPHORES = (["a%d" % i for i in range(N)] + ["pb%d" % i for i in range(N)] + ["vx%d" % i for i in range(N)] +
+              ["sent", "ld_wd", "ld_w", "ld_x", "ld_rt", "ld_rm", "c1", "c2", "c3", "p1", "p2", "p3", "py",
+               "v1", "v2", "v3", "v4", "v5", "v6", "v7", "a_e", "st"])
+
+_CACHE = {}
+
+
+def _plan(ranks, topo):
+    if "plan" in _CACHE:
+        return _CACHE["plan"]
+
+    def ck(c):
+        return (topo.host(c), topo.chip(c))
+
+    def links(a, b):
+        if ck(a) == ck(b):
+            return 0
+        if topo.rack(topo.host(a)) == topo.rack(topo.host(b)):
+            return 1 if (topo.mates(a, b) or topo.same_plane(a, b)) else 2
+        if topo.chip(a) == topo.chip(b):
+            return 1
+        img = [c for c in range(NSIM) if topo.host(c) == topo.host(a) and topo.chip(c) == topo.chip(b)][0]
+        return 1 + links(a, img)
+
+    helpers = [c for c in range(NSIM) if c not in ranks and any(ck(c) == ck(r) for r in ranks)]
+    reach = {h: sum(1 for r in ranks if topo.may_write(h, r)) for h in helpers}
+    used, chipload, dieload, out = {}, {}, {}, {}
+    for s in ranks:
+        direct = [d for d in ranks if d != s and topo.may_write(s, d) and links(s, d) <= 2]
+        groups = {}
+        for d in ranks:
+            if d != s and d not in direct:
+                groups.setdefault(ck(d), []).append(d)
+        relays = []
+        for grp in sorted(groups.values(), key=lambda q: -len(q)):
+            def cost(h):
+                a, b = links(s, h), max(links(h, d) for d in grp)
+                return (a + b, max(a, b))
+
+            def ok(h):
+                return topo.may_write(s, h) and all(topo.may_write(h, d) for d in grp)
+
+            cand = [h for h in helpers if h not in used and ok(h)]
+            best = min(cost(h) for h in cand)
+            join = [r for r in relays if len(r[1]) + len(grp) <= 2 and ok(r[0]) and cost(r[0]) <= best]
+            if join:
+                join[0][1].extend(grp)
+                continue
+            cand = [h for h in cand if cost(h) == best]
+            h = min(cand, key=lambda q: (reach[q], chipload.get(ck(q), 0), dieload.get((ck(q), topo.die(q)), 0), q))
+            used[h] = s
+            chipload[ck(h)] = chipload.get(ck(h), 0) + 1
+            dieload[(ck(h), topo.die(h))] = dieload.get((ck(h), topo.die(h)), 0) + 1
+            relays.append([h, list(grp)])
+        relays.sort(key=lambda r: (-len(r[1]), -links(s, r[0])))
+        direct.sort(key=lambda d: -links(s, d))
+        out[s] = (direct, relays)
+    _CACHE["plan"] = out
+    return out
+
+
+def _send(g, core, topo, src, dst_ap, dests, sem, local_sem):
+    mask = topo.mask(core, dests[0])
+    for d in dests:
+        mask &= topo.mask(core, d)
+    ids = []
+    for d in dests:
+        rid, pid = topo.addr(d, core)
+        ids.append(DstId(rid=rid, pnc=pid))
+    g.remote_dma_fused([RemoteDMATransfer(dst_ids=ids, dma_engine_mask=mask, remote_sem=sem,
+                                          srcs=[src], dsts=[dst_ap for _ in dests])], local_sem=local_sem)
+    return bin(mask).count("1")
+
+
+def _engines(topo, a, dests):
+    mask = topo.mask(a, dests[0])
+    for d in dests:
+        mask &= topo.mask(a, d)
+    return bin(mask).count("1")
+
+
+def rank_program(g, core, T, topo):
+    ranks = list(T.cores)
+    plan = _plan(ranks, topo)
+    rank = T.rank_of(core)
+    S = T.sem
+
+    if rank is None:
+        for s in ranks:
+            feeds = [r[0] for r in plan[s][1]]
+            for h, dests in plan[s][1]:
+                if h == core:
+                    e = ranks.index(s)
+                    g.wait_ge(S["a%d" % e], _engines(topo, s, feeds))
+                    n = _send(g, core, topo, T.wd[:], T.wall[:, e * D:(e + 1) * D], dests, S["a%d" % e], S.sent)
+                    g.wait_ge(S.sent, n)
+        return
+
+    direct, relays = plan[core]
+    own = T.wall[:, rank * D:(rank + 1) * D]
+
+    g.sync.dma_start(T.wd[:], T.w[:]).then_inc(S.ld_wd, 16)
+    g.scalar.dma_start(T.xs[:], T.x[:]).then_inc(S.ld_x, 16)
+    g.scalar.dma_start(T.rts[:], T.rt[:]).then_inc(S.ld_rt, 16)
+    g.sync.dma_start(T.rms[0:N, :], T.rm[:]).then_inc(S.ld_rm, 16)
+    g.sync.dma_start(own, T.w[:]).then_inc(S.ld_w, 16)
+
+    V, P, A = g.vector, g.tensor, g.scalar
+    V.memset(T.ones[:], 1.0).then_inc(S.c1, 1)
+    g.wait_ge(S.c1, 1)
+    g.affine_select(T.ident[:], T.ones[:], [[-1, 128]], AluOpType.is_equal, 0.0, 0, 1).then_inc(S.c2, 1)
+
+    g.wait_ge(S.ld_wd, 16)
+    sent = _send(g, core, topo, T.wd[:], T.wd[:], [r[0] for r in relays], S["a%d" % rank], S.sent)
+    sent += _send(g, core, topo, T.wd[:], own, direct, S["a%d" % rank], S.sent)
+
+    when = {rank: ((-1, 0, 0), 0)}
+    for e, s in enumerate(ranks):
+        if s == core:
+            continue
+        dl, rl = plan[s]
+        if core in dl:
+            when[e] = ((0, dl.index(core), 0), _engines(topo, s, dl))
+        for i, (h, dests) in enumerate(rl):
+            if core in dests:
+                when[e] = ((1, dests.index(core), i), _engines(topo, h, dests))
+    order = sorted(range(N), key=lambda e: when[e][0])
+
+    V.wait_ge(S.c2, 1)
+    for e in range(N):
+        V.tensor_scalar(T.sel[0:N, e * D:(e + 1) * D], T.ones[0:N, 0:D], T.ident[0:N, e:e + 1], None,
+                        AluOpType.mult).then_inc(S.c3, 1)
+
+    P.wait_ge(S.ld_x, 16)
+    P.wait_ge(S.ld_rt, 16)
+    for h in range(2):
+        P.matmul(T.ps_s[:, h * N:(h + 1) * N], T.xs[:, h * 128:(h + 1) * 128], T.rts[:], True, True).then_inc(S.p1, 1)
+    P.wait_ge(S.ld_rm, 16)
+    P.wait_ge(S.c2, 1)
+    for h in range(2):
+        P.matmul(T.ps_m[:, h * N:(h + 1) * N], T.rms[0:N, h * 128:(h + 1) * 128], T.ident[0:N, 0:N], True,
+                 True).then_inc(S.p2, 1)
+
+    V.wait_ge(S.p2, 2)
+    V.tensor_scalar(T.pen[:], T.ps_m[:, 0:2 * N], 2.0 * BIG, -BIG, AluOpType.mult, AluOpType.add).then_inc(S.v1, 1)
+    V.wait_ge(S.p1, 2)
+    V.wait_ge(S.v1, 1)
+    V.tensor_tensor(T.msk[:], T.ps_s[:, 0:2 * N], T.pen[:], AluOpType.min).then_inc(S.v2, 1)
+    V.wait_ge(S.v2, 1)
+    for h in range(2):
+        V.tensor_reduce(T.negm[:, h:h + 1], T.msk[:, h * N:(h + 1) * N], AxisListType.X, AluOpType.max,
+                        negate=True).then_inc(S.v3, 1)
+    A.wait_ge(S.v3, 2)
+    for h in range(2):
+        A.activation(T.ex[:, h * N:(h + 1) * N], T.msk[:, h * N:(h + 1) * N], ActivationFunctionType.Exp,
+                     bias=T.negm[:, h:h + 1], scale=1.0, accum_out=T.ssum[:, h:h + 1]).then_inc(S.a_e, 1)
+    V.wait_ge(S.a_e, 2)
+    V.reciprocal(T.rs[:], T.ssum[:]).then_inc(S.v4, 1)
+    V.wait_ge(S.v4, 1)
+    for h in range(2):
+        V.tensor_scalar(T.gt[:, h * N:(h + 1) * N], T.ex[:, h * N:(h + 1) * N], T.rs[:, h:h + 1], None,
+                        AluOpType.mult).then_inc(S.v5, 1)
+
+    P.wait_ge(S.v5, 2)
+    for h in range(2):
+        P.matmul(T.ps_g[0:N, h * 128:(h + 1) * 128], T.gt[:, h * N:(h + 1) * N], T.ident[:], True, True).then_inc(S.p3, 1)
+    V.wait_ge(S.p3, 2)
+    V.tensor_copy(T.g10[0:N, :], T.ps_g[0:N, 0:TOK]).then_inc(S.v6, 1)
+    P.wait_ge(S.v6, 1)
+    P.wait_ge(S.c3, N)
+    V.wait_ge(S.ld_x, 16)
+    for i, e in enumerate(order):
+        bank = T["ps_b%d" % (i % NB)]
+        if i >= NB:
+            P.wait_ge(S["vx%d" % order[i - NB]], 1)
+        P.matmul(bank[:, 0:TOK], T.sel[0:N, e * D:(e + 1) * D], T.g10[0:N, :], True, True).then_inc(S["pb%d" % e], 1)
+        V.wait_ge(S["pb%d" % e], 1)
+        V.tensor_tensor(T.xg[:, e * TOK:(e + 1) * TOK], bank[:, 0:TOK], T.xs[:], AluOpType.mult).then_inc(S["vx%d" % e], 1)
+
+    for i, e in enumerate(order):
+        P.wait_ge(S["vx%d" % e], 1)
+        if e == rank:
+            P.wait_ge(S.ld_w, 16)
+        else:
+            P.wait_ge(S["a%d" % e], when[e][1])
+        mm = P.matmul(T.ps_y[:, 0:TOK], T.wall[:, e * D:(e + 1) * D], T.xg[:, e * TOK:(e + 1) * TOK], i == 0, i == N - 1)
+        if i == N - 1:
+            mm.then_inc(S.py, 1)
+    V.wait_ge(S.py, 1)
+    V.tensor_copy(T.ys[:], T.ps_y[:, 0:TOK]).then_inc(S.v7, 1)
+    g.sync.wait_ge(S.v7, 1)
+    g.sync.dma_start(T.y[:], T.ys[:]).then_inc(S.st, 16)
+    g.sync.wait_ge(S.st, 16)
+    g.wait_ge(S.sent, sent)

@@ -13,6 +13,8 @@ SCRATCH = {
     "rts": ("sbuf", [128, N], "bfloat16"),
     "rms": ("sbuf", [128, TOK], "bfloat16"),
     "ones": ("sbuf", [128, 128], "bfloat16"),
+    "zer": ("sbuf", [128, 128], "bfloat16"),
+    "one2": ("sbuf", [128, 128], "bfloat16"),
     "ident": ("sbuf", [128, 128], "bfloat16"),
     "sel": ("sbuf", [128, N * D], "bfloat16"),
     "pen": ("sbuf", [128, 2 * N], "float32"),
@@ -35,10 +37,18 @@ SCRATCH = {
     "ps_b3": ("psum", [128, 512], "float32"),
 }
 SEMAPHORES = (["a%d" % i for i in range(N)] + ["pb%d" % i for i in range(N)] + ["vx%d" % i for i in range(N)] +
-              ["sent", "ld_wd", "ld_w", "ld_x", "ld_rt", "ld_rm", "c1", "c2", "c3", "p1", "p2", "p3", "py",
-               "v1", "v2", "v3", "v4", "v5", "v6", "v7", "a_e", "st"])
+              ["sent", "sl", "ld_wd", "ld_w", "ld_x", "ld_rt", "ld_rm", "c0", "c1", "c2", "c3", "p1", "p2", "p3", "py",
+               "v1", "v2", "v3", "v4", "v5", "v6", "v7", "a_z", "a_e", "st"])
 
 _CACHE = {}
+
+
+def _ck(topo, c):
+    return (topo.host(c), topo.chip(c))
+
+
+def _bits(m):
+    return bin(m).count("1")
 
 
 def _plan(ranks, topo):
@@ -46,7 +56,7 @@ def _plan(ranks, topo):
         return _CACHE["plan"]
 
     def ck(c):
-        return (topo.host(c), topo.chip(c))
+        return _ck(topo, c)
 
     def links(a, b):
         if ck(a) == ck(b):
@@ -60,7 +70,7 @@ def _plan(ranks, topo):
 
     helpers = [c for c in range(NSIM) if c not in ranks and any(ck(c) == ck(r) for r in ranks)]
     reach = {h: sum(1 for r in ranks if topo.may_write(h, r)) for h in helpers}
-    used, chipload, dieload, out = {}, {}, {}, {}
+    used, chipload, dieload, inload, out = {}, {}, {}, {}, {}
     for s in ranks:
         direct = [d for d in ranks if d != s and topo.may_write(s, d) and links(s, d) <= 2]
         groups = {}
@@ -76,64 +86,151 @@ def _plan(ranks, topo):
             def ok(h):
                 return topo.may_write(s, h) and all(topo.may_write(h, d) for d in grp)
 
+            def port(h):
+                return sum(inload.get((ck(d), topo.die(h)), 0) for d in grp if ck(d) != ck(h))
+
             cand = [h for h in helpers if h not in used and ok(h)]
             best = min(cost(h) for h in cand)
             join = [r for r in relays if len(r[1]) + len(grp) <= 2 and ok(r[0]) and cost(r[0]) <= best]
             if join:
+                h = join[0][0]
                 join[0][1].extend(grp)
-                continue
-            cand = [h for h in cand if cost(h) == best]
-            h = min(cand, key=lambda q: (reach[q], chipload.get(ck(q), 0), dieload.get((ck(q), topo.die(q)), 0), q))
-            used[h] = s
-            chipload[ck(h)] = chipload.get(ck(h), 0) + 1
-            dieload[(ck(h), topo.die(h))] = dieload.get((ck(h), topo.die(h)), 0) + 1
-            relays.append([h, list(grp)])
+            else:
+                cand = [h for h in cand if cost(h) == best]
+                h = min(cand, key=lambda q: (reach[q], chipload.get(ck(q), 0), port(q),
+                                             dieload.get((ck(q), topo.die(q)), 0), q))
+                used[h] = s
+                chipload[ck(h)] = chipload.get(ck(h), 0) + 1
+                dieload[(ck(h), topo.die(h))] = dieload.get((ck(h), topo.die(h)), 0) + 1
+                relays.append([h, list(grp)])
+            for d in grp:
+                inload[(ck(d), topo.die(h))] = inload.get((ck(d), topo.die(h)), 0) + 1
         relays.sort(key=lambda r: (-len(r[1]), -links(s, r[0])))
         direct.sort(key=lambda d: -links(s, d))
-        out[s] = (direct, relays)
+        rl = [[h, [d for d in ds if ck(d) != ck(h)], [d for d in ds if ck(d) == ck(h)]] for h, ds in relays]
+        for d in list(direct):
+            c = [r for r in rl if ck(r[0]) == ck(d)]
+            if c:
+                min(c, key=lambda r: len(r[1]) + len(r[2]))[2].append(d)
+                direct.remove(d)
+        out[s] = (direct, rl)
     _CACHE["plan"] = out
     return out
 
 
-def _send(g, core, topo, src, dst_ap, dests, sem, local_sem):
-    mask = topo.mask(core, dests[0])
-    for d in dests:
-        mask &= topo.mask(core, d)
-    ids = []
-    for d in dests:
-        rid, pid = topo.addr(d, core)
-        ids.append(DstId(rid=rid, pnc=pid))
-    g.remote_dma_fused([RemoteDMATransfer(dst_ids=ids, dma_engine_mask=mask, remote_sem=sem,
-                                          srcs=[src], dsts=[dst_ap for _ in dests])], local_sem=local_sem)
-    return bin(mask).count("1")
+def _masks(topo, core, off, on):
+    moff, mon = 0, 0
+    if off:
+        moff = topo.mask(core, off[0])
+        for d in off:
+            moff &= topo.mask(core, d)
+    if on:
+        mon = topo.mask(core, on[0])
+        for d in on:
+            mon &= topo.mask(core, d)
+        mon &= ~moff
+    return moff, mon
 
 
-def _engines(topo, a, dests):
-    mask = topo.mask(a, dests[0])
-    for d in dests:
-        mask &= topo.mask(a, d)
-    return bin(mask).count("1")
+def _src_sets(topo, plan, s):
+    direct, rl = plan[s]
+    f_off = [r[0] for r in rl if _ck(topo, r[0]) != _ck(topo, s)]
+    f_on = [r[0] for r in rl if _ck(topo, r[0]) == _ck(topo, s)]
+    d_off = [d for d in direct if _ck(topo, d) != _ck(topo, s)]
+    d_on = [d for d in direct if _ck(topo, d) == _ck(topo, s)]
+    return f_off, f_on, d_off, d_on
+
+
+def _arrivals(ranks, topo, plan, core):
+    when = {ranks.index(core): ((-1, 0, 0), 0)}
+    for e, s in enumerate(ranks):
+        if s == core:
+            continue
+        f_off, f_on, d_off, d_on = _src_sets(topo, plan, s)
+        moff, mon = _masks(topo, s, f_off + d_off, f_on + d_on)
+        if core in d_on:
+            when[e] = ((0, 0, d_on.index(core)), _bits(mon))
+        if core in d_off:
+            when[e] = ((0, 1, d_off.index(core)), _bits(moff))
+        for h, off, on in plan[s][1]:
+            place = f_off.index(h) if h in f_off else len(f_off) + f_on.index(h)
+            ro, rn = _masks(topo, h, off, on)
+            if core in on:
+                when[e] = ((1, on.index(core), place), _bits(rn))
+            if core in off:
+                when[e] = ((1, off.index(core), place), _bits(ro))
+    return when, sorted(range(N), key=lambda e: when[e][0])
+
+
+def _brought(ranks, topo, plan):
+    if "brought" in _CACHE:
+        return _CACHE["brought"]
+    out, chips = {}, {}
+    for s in ranks:
+        for r in plan[s][1]:
+            chips.setdefault(_ck(topo, r[0]), []).append(r[0])
+    for c, hs in chips.items():
+        here = [r for r in ranks if _ck(topo, r) == c]
+        for j, h in enumerate(sorted(hs)):
+            r = here[j % len(here)]
+            order = _arrivals(ranks, topo, plan, r)[1]
+            out[h] = (r, order[N - 1 - j // len(here)])
+    _CACHE["brought"] = out
+    return out
+
+
+def _call(g, core, topo, parts, sem, local_sem):
+    trs, n = [], 0
+    for mask, src, dd in parts:
+        if not dd:
+            continue
+        ids = []
+        for d, _ in dd:
+            rid, pid = topo.addr(d, core)
+            ids.append(DstId(rid=rid, pnc=pid))
+        trs.append(RemoteDMATransfer(dst_ids=ids, dma_engine_mask=mask, remote_sem=sem,
+                                     srcs=[src], dsts=[ap for _, ap in dd]))
+        n += _bits(mask)
+    if trs:
+        g.remote_dma_fused(trs, local_sem=local_sem)
+    return n
 
 
 def rank_program(g, core, T, topo):
     ranks = list(T.cores)
     plan = _plan(ranks, topo)
+    brought = _brought(ranks, topo, plan)
     rank = T.rank_of(core)
     S = T.sem
 
     if rank is None:
         for s in ranks:
-            feeds = [r[0] for r in plan[s][1]]
-            for h, dests in plan[s][1]:
-                if h == core:
-                    e = ranks.index(s)
-                    g.wait_ge(S["a%d" % e], _engines(topo, s, feeds))
-                    n = _send(g, core, topo, T.wd[:], T.wall[:, e * D:(e + 1) * D], dests, S["a%d" % e], S.sent)
-                    g.wait_ge(S.sent, n)
+            for h, off, on in plan[s][1]:
+                if h != core:
+                    continue
+                e = ranks.index(s)
+                r, b = brought[core]
+                g.vector.memset(T.ones[:], 1.0).then_inc(S.c1, 1)
+                g.wait_ge(S.c1, 1)
+                g.affine_select(T.ident[:], T.ones[:], [[0, 128]], AluOpType.is_equal, 0.0, -b, 1).then_inc(S.c2, 1)
+                g.wait_ge(S.c2, 1)
+                n = _call(g, core, topo, [(topo.mask(core, r), T.ident[:], [(r, T.sel[:, b * D:(b + 1) * D])])],
+                          S.sl, S.sent)
+                f_off, f_on, d_off, d_on = _src_sets(topo, plan, s)
+                moff, mon = _masks(topo, s, f_off + d_off, f_on + d_on)
+                g.wait_ge(S["a%d" % e], _bits(moff if core in f_off else mon))
+                ro, rn = _masks(topo, core, off, on)
+                slot = T.wall[:, e * D:(e + 1) * D]
+                n += _call(g, core, topo, [(ro, T.wd[:], [(d, slot) for d in off]),
+                                           (rn, T.wd[:], [(d, slot) for d in on])], S["a%d" % e], S.sent)
+                g.wait_ge(S.sent, n)
         return
 
-    direct, relays = plan[core]
     own = T.wall[:, rank * D:(rank + 1) * D]
+    when, order = _arrivals(ranks, topo, plan, core)
+    got = [(h, b) for h, (r, b) in sorted(brought.items()) if r == core]
+    got_e = [b for _, b in got]
+    got_n = sum(_bits(topo.mask(h, core)) for h, _ in got)
 
     g.sync.dma_start(T.wd[:], T.w[:]).then_inc(S.ld_wd, 16)
     g.scalar.dma_start(T.xs[:], T.x[:]).then_inc(S.ld_x, 16)
@@ -143,29 +240,19 @@ def rank_program(g, core, T, topo):
 
     V, P, A = g.vector, g.tensor, g.scalar
     V.memset(T.ones[:], 1.0).then_inc(S.c1, 1)
+    V.memset(T.zer[0:N, 0:D], 0.0).then_inc(S.c0, 1)
     g.wait_ge(S.c1, 1)
     g.affine_select(T.ident[:], T.ones[:], [[-1, 128]], AluOpType.is_equal, 0.0, 0, 1).then_inc(S.c2, 1)
+    A.wait_ge(S.c0, 1)
+    A.activation(T.one2[0:N, 0:D], T.zer[0:N, 0:D], ActivationFunctionType.Exp).then_inc(S.a_z, 1)
 
+    f_off, f_on, d_off, d_on = _src_sets(topo, plan, core)
+    moff, mon = _masks(topo, core, f_off + d_off, f_on + d_on)
     g.wait_ge(S.ld_wd, 16)
-    sent = _send(g, core, topo, T.wd[:], T.wd[:], [r[0] for r in relays], S["a%d" % rank], S.sent)
-    sent += _send(g, core, topo, T.wd[:], own, direct, S["a%d" % rank], S.sent)
-
-    when = {rank: ((-1, 0, 0), 0)}
-    for e, s in enumerate(ranks):
-        if s == core:
-            continue
-        dl, rl = plan[s]
-        if core in dl:
-            when[e] = ((0, dl.index(core), 0), _engines(topo, s, dl))
-        for i, (h, dests) in enumerate(rl):
-            if core in dests:
-                when[e] = ((1, dests.index(core), i), _engines(topo, h, dests))
-    order = sorted(range(N), key=lambda e: when[e][0])
-
-    V.wait_ge(S.c2, 1)
-    for e in range(N):
-        V.tensor_scalar(T.sel[0:N, e * D:(e + 1) * D], T.ones[0:N, 0:D], T.ident[0:N, e:e + 1], None,
-                        AluOpType.mult).then_inc(S.c3, 1)
+    sent = _call(g, core, topo, [(moff, T.wd[:], [(h, T.wd[:]) for h in f_off])], S["a%d" % rank], S.sent)
+    sent += _call(g, core, topo, [(moff, T.wd[:], [(d, own) for d in d_off]),
+                                  (mon, T.wd[:], [(h, T.wd[:]) for h in f_on] + [(d, own) for d in d_on])],
+                  S["a%d" % rank], S.sent)
 
     P.wait_ge(S.ld_x, 16)
     P.wait_ge(S.ld_rt, 16)
@@ -190,6 +277,12 @@ def rank_program(g, core, T, topo):
     for h in range(2):
         A.activation(T.ex[:, h * N:(h + 1) * N], T.msk[:, h * N:(h + 1) * N], ActivationFunctionType.Exp,
                      bias=T.negm[:, h:h + 1], scale=1.0, accum_out=T.ssum[:, h:h + 1]).then_inc(S.a_e, 1)
+    V.wait_ge(S.c2, 1)
+    V.wait_ge(S.a_z, 1)
+    made = [e for e in range(N) if e not in got_e]
+    for e in made:
+        V.tensor_scalar(T.sel[0:N, e * D:(e + 1) * D], T.one2[0:N, 0:D], T.ident[0:N, e:e + 1], None,
+                        AluOpType.mult).then_inc(S.c3, 1)
     V.wait_ge(S.a_e, 2)
     V.reciprocal(T.rs[:], T.ssum[:]).then_inc(S.v4, 1)
     V.wait_ge(S.v4, 1)
@@ -203,12 +296,16 @@ def rank_program(g, core, T, topo):
     V.wait_ge(S.p3, 2)
     V.tensor_copy(T.g10[0:N, :], T.ps_g[0:N, 0:TOK]).then_inc(S.v6, 1)
     P.wait_ge(S.v6, 1)
-    P.wait_ge(S.c3, N)
+    P.wait_ge(S.c3, len(made))
     V.wait_ge(S.ld_x, 16)
+    waited = False
     for i, e in enumerate(order):
         bank = T["ps_b%d" % (i % NB)]
         if i >= NB:
             P.wait_ge(S["vx%d" % order[i - NB]], 1)
+        if e in got_e and not waited:
+            P.wait_ge(S.sl, got_n)
+            waited = True
         P.matmul(bank[:, 0:TOK], T.sel[0:N, e * D:(e + 1) * D], T.g10[0:N, :], True, True).then_inc(S["pb%d" % e], 1)
         V.wait_ge(S["pb%d" % e], 1)
         V.tensor_tensor(T.xg[:, e * TOK:(e + 1) * TOK], bank[:, 0:TOK], T.xs[:], AluOpType.mult).then_inc(S["vx%d" % e], 1)

from concourse.bass import DstId, RemoteDMATransfer
from concourse.mybir import AluOpType, AxisListType, ActivationFunctionType

NSIM = 512
N, TOK, D = 10, 256, 128
BIG = 1e29
NB = 4

SCRATCH = {
    "wd": ("dram", [128, 128], "bfloat16"),
    "wall": ("sbuf", [128, N * D], "bfloat16"),
    "xs": ("sbuf", [128, TOK], "bfloat16"),
    "rts": ("sbuf", [128, N], "bfloat16"),
    "rms": ("sbuf", [128, TOK], "bfloat16"),
    "ones": ("sbuf", [128, 128], "bfloat16"),
    "zer": ("sbuf", [128, 128], "bfloat16"),
    "one2": ("sbuf", [128, 128], "bfloat16"),
    "ident": ("sbuf", [128, 128], "bfloat16"),
    "sel": ("sbuf", [128, N * D], "bfloat16"),
    "pen": ("sbuf", [128, 2 * N], "float32"),
    "msk": ("sbuf", [128, 2 * N], "float32"),
    "negm": ("sbuf", [128, 2], "float32"),
    "ex": ("sbuf", [128, 2 * N], "float32"),
    "ssum": ("sbuf", [128, 2], "float32"),
    "rs": ("sbuf", [128, 2], "float32"),
    "gt": ("sbuf", [128, 2 * N], "bfloat16"),
    "g10": ("sbuf", [128, TOK], "bfloat16"),
    "xg": ("sbuf", [128, N * TOK], "bfloat16"),
    "ys": ("sbuf", [128, TOK], "bfloat16"),
    "ps_s": ("psum", [128, 512], "float32"),
    "ps_m": ("psum", [128, 512], "float32"),
    "ps_g": ("psum", [128, 512], "float32"),
    "ps_y": ("psum", [128, 512], "float32"),
    "ps_b0": ("psum", [128, 512], "float32"),
    "ps_b1": ("psum", [128, 512], "float32"),
    "ps_b2": ("psum", [128, 512], "float32"),
    "ps_b3": ("psum", [128, 512], "float32"),
}
SEMAPHORES = (["a%d" % i for i in range(N)] + ["pb%d" % i for i in range(N)] + ["vx%d" % i for i in range(N)] +
              ["sent", "sl", "ld_wd", "ld_w", "ld_x", "ld_rt", "ld_rm", "c0", "c1", "c2", "c3", "p1", "p2", "p3", "py",
               "v1", "v2", "v3", "v4", "v5", "v6", "v7", "a_z", "a_e", "st"])

_CACHE = {}


def _ck(topo, c):
    return (topo.host(c), topo.chip(c))


def _bits(m):
    return bin(m).count("1")


def _plan(ranks, topo):
    if "plan" in _CACHE:
        return _CACHE["plan"]

    def ck(c):
        return _ck(topo, c)

    def links(a, b):
        if ck(a) == ck(b):
            return 0
        if topo.rack(topo.host(a)) == topo.rack(topo.host(b)):
            return 1 if (topo.mates(a, b) or topo.same_plane(a, b)) else 2
        if topo.chip(a) == topo.chip(b):
            return 1
        img = [c for c in range(NSIM) if topo.host(c) == topo.host(a) and topo.chip(c) == topo.chip(b)][0]
        return 1 + links(a, img)

    helpers = [c for c in range(NSIM) if c not in ranks and any(ck(c) == ck(r) for r in ranks)]
    reach = {h: sum(1 for r in ranks if topo.may_write(h, r)) for h in helpers}
    used, chipload, dieload, inload, out = {}, {}, {}, {}, {}
    for s in ranks:
        direct = [d for d in ranks if d != s and topo.may_write(s, d) and links(s, d) <= 2]
        groups = {}
        for d in ranks:
            if d != s and d not in direct:
                groups.setdefault(ck(d), []).append(d)
        relays = []
        for grp in sorted(groups.values(), key=lambda q: -len(q)):
            def cost(h):
                a, b = links(s, h), max(links(h, d) for d in grp)
                return (a + b, max(a, b))

            def ok(h):
                return topo.may_write(s, h) and all(topo.may_write(h, d) for d in grp)

            def port(h):
                return sum(inload.get((ck(d), topo.die(h)), 0) for d in grp if ck(d) != ck(h))

            cand = [h for h in helpers if h not in used and ok(h)]
            best = min(cost(h) for h in cand)
            join = [r for r in relays if len(r[1]) + len(grp) <= 2 and ok(r[0]) and cost(r[0]) <= best]
            if join:
                h = join[0][0]
                join[0][1].extend(grp)
            else:
                cand = [h for h in cand if cost(h) == best]
                h = min(cand, key=lambda q: (reach[q], chipload.get(ck(q), 0), port(q),
                                             dieload.get((ck(q), topo.die(q)), 0), q))
                used[h] = s
                chipload[ck(h)] = chipload.get(ck(h), 0) + 1
                dieload[(ck(h), topo.die(h))] = dieload.get((ck(h), topo.die(h)), 0) + 1
                relays.append([h, list(grp)])
            for d in grp:
                inload[(ck(d), topo.die(h))] = inload.get((ck(d), topo.die(h)), 0) + 1
        relays.sort(key=lambda r: (-len(r[1]), -links(s, r[0])))
        direct.sort(key=lambda d: -links(s, d))
        rl = [[h, [d for d in ds if ck(d) != ck(h)], [d for d in ds if ck(d) == ck(h)]] for h, ds in relays]
        for d in list(direct):
            c = [r for r in rl if ck(r[0]) == ck(d)]
            if c:
                min(c, key=lambda r: len(r[1]) + len(r[2]))[2].append(d)
                direct.remove(d)
        out[s] = (direct, rl)
    _CACHE["plan"] = out
    return out


def _masks(topo, core, off, on):
    moff, mon = 0, 0
    if off:
        moff = topo.mask(core, off[0])
        for d in off:
            moff &= topo.mask(core, d)
    if on:
        mon = topo.mask(core, on[0])
        for d in on:
            mon &= topo.mask(core, d)
        mon &= ~moff
    return moff, mon


def _src_sets(topo, plan, s):
    direct, rl = plan[s]
    f_off = [r[0] for r in rl if _ck(topo, r[0]) != _ck(topo, s)]
    f_on = [r[0] for r in rl if _ck(topo, r[0]) == _ck(topo, s)]
    d_off = [d for d in direct if _ck(topo, d) != _ck(topo, s)]
    d_on = [d for d in direct if _ck(topo, d) == _ck(topo, s)]
    return f_off, f_on, d_off, d_on


def _arrivals(ranks, topo, plan, core):
    when = {ranks.index(core): ((-1, 0, 0), 0)}
    for e, s in enumerate(ranks):
        if s == core:
            continue
        f_off, f_on, d_off, d_on = _src_sets(topo, plan, s)
        moff, mon = _masks(topo, s, f_off + d_off, f_on + d_on)
        if core in d_on:
            when[e] = ((0, 0, d_on.index(core)), _bits(mon))
        if core in d_off:
            when[e] = ((0, 1, d_off.index(core)), _bits(moff))
        for h, off, on in plan[s][1]:
            place = f_off.index(h) if h in f_off else len(f_off) + f_on.index(h)
            ro, rn = _masks(topo, h, off, on)
            if core in on:
                when[e] = ((1, on.index(core), place), _bits(rn))
            if core in off:
                when[e] = ((1, off.index(core), place), _bits(ro))
    return when, sorted(range(N), key=lambda e: when[e][0])


def _brought(ranks, topo, plan):
    if "brought" in _CACHE:
        return _CACHE["brought"]
    out, chips = {}, {}
    for s in ranks:
        for r in plan[s][1]:
            chips.setdefault(_ck(topo, r[0]), []).append(r[0])
    for c, hs in chips.items():
        here = [r for r in ranks if _ck(topo, r) == c]
        for j, h in enumerate(sorted(hs)):
            r = here[j % len(here)]
            order = _arrivals(ranks, topo, plan, r)[1]
            out[h] = (r, order[N - 1 - j // len(here)])
    _CACHE["brought"] = out
    return out


def _call(g, core, topo, parts, sem, local_sem):
    trs, n = [], 0
    for mask, src, dd in parts:
        if not dd:
            continue
        ids = []
        for d, _ in dd:
            rid, pid = topo.addr(d, core)
            ids.append(DstId(rid=rid, pnc=pid))
        trs.append(RemoteDMATransfer(dst_ids=ids, dma_engine_mask=mask, remote_sem=sem,
                                     srcs=[src], dsts=[ap for _, ap in dd]))
        n += _bits(mask)
    if trs:
        g.remote_dma_fused(trs, local_sem=local_sem)
    return n


def rank_program(g, core, T, topo):
    ranks = list(T.cores)
    plan = _plan(ranks, topo)
    brought = _brought(ranks, topo, plan)
    rank = T.rank_of(core)
    S = T.sem

    if rank is None:
        for s in ranks:
            for h, off, on in plan[s][1]:
                if h != core:
                    continue
                e = ranks.index(s)
                r, b = brought[core]
                g.vector.memset(T.ones[:], 1.0).then_inc(S.c1, 1)
                g.wait_ge(S.c1, 1)
                g.affine_select(T.ident[:], T.ones[:], [[0, 128]], AluOpType.is_equal, 0.0, -b, 1).then_inc(S.c2, 1)
                g.wait_ge(S.c2, 1)
                n = _call(g, core, topo, [(topo.mask(core, r), T.ident[:], [(r, T.sel[:, b * D:(b + 1) * D])])],
                          S.sl, S.sent)
                f_off, f_on, d_off, d_on = _src_sets(topo, plan, s)
                moff, mon = _masks(topo, s, f_off + d_off, f_on + d_on)
                g.wait_ge(S["a%d" % e], _bits(moff if core in f_off else mon))
                ro, rn = _masks(topo, core, off, on)
                slot = T.wall[:, e * D:(e + 1) * D]
                n += _call(g, core, topo, [(ro, T.wd[:], [(d, slot) for d in off]),
                                           (rn, T.wd[:], [(d, slot) for d in on])], S["a%d" % e], S.sent)
                g.wait_ge(S.sent, n)
        return

    own = T.wall[:, rank * D:(rank + 1) * D]
    when, order = _arrivals(ranks, topo, plan, core)
    got = [(h, b) for h, (r, b) in sorted(brought.items()) if r == core]
    got_e = [b for _, b in got]
    got_n = sum(_bits(topo.mask(h, core)) for h, _ in got)

    g.sync.dma_start(T.wd[:], T.w[:]).then_inc(S.ld_wd, 16)
    g.scalar.dma_start(T.xs[:], T.x[:]).then_inc(S.ld_x, 16)
    g.scalar.dma_start(T.rts[:], T.rt[:]).then_inc(S.ld_rt, 16)
    g.sync.dma_start(T.rms[0:N, :], T.rm[:]).then_inc(S.ld_rm, 16)
    g.sync.dma_start(own, T.w[:]).then_inc(S.ld_w, 16)

    V, P, A = g.vector, g.tensor, g.scalar
    V.memset(T.ones[:], 1.0).then_inc(S.c1, 1)
    V.memset(T.zer[0:N, 0:D], 0.0).then_inc(S.c0, 1)
    g.wait_ge(S.c1, 1)
    g.affine_select(T.ident[:], T.ones[:], [[-1, 128]], AluOpType.is_equal, 0.0, 0, 1).then_inc(S.c2, 1)
    A.wait_ge(S.c0, 1)
    A.activation(T.one2[0:N, 0:D], T.zer[0:N, 0:D], ActivationFunctionType.Exp).then_inc(S.a_z, 1)

    f_off, f_on, d_off, d_on = _src_sets(topo, plan, core)
    moff, mon = _masks(topo, core, f_off + d_off, f_on + d_on)
    g.wait_ge(S.ld_wd, 16)
    sent = _call(g, core, topo, [(moff, T.wd[:], [(h, T.wd[:]) for h in f_off])], S["a%d" % rank], S.sent)
    sent += _call(g, core, topo, [(moff, T.wd[:], [(d, own) for d in d_off]),
                                  (mon, T.wd[:], [(h, T.wd[:]) for h in f_on] + [(d, own) for d in d_on])],
                  S["a%d" % rank], S.sent)

    P.wait_ge(S.ld_x, 16)
    P.wait_ge(S.ld_rt, 16)
    for h in range(2):
        P.matmul(T.ps_s[:, h * N:(h + 1) * N], T.xs[:, h * 128:(h + 1) * 128], T.rts[:], True, True).then_inc(S.p1, 1)
    P.wait_ge(S.ld_rm, 16)
    P.wait_ge(S.c2, 1)
    for h in range(2):
        P.matmul(T.ps_m[:, h * N:(h + 1) * N], T.rms[0:N, h * 128:(h + 1) * 128], T.ident[0:N, 0:N], True,
                 True).then_inc(S.p2, 1)

    V.wait_ge(S.p2, 2)
    V.tensor_scalar(T.pen[:], T.ps_m[:, 0:2 * N], 2.0 * BIG, -BIG, AluOpType.mult, AluOpType.add).then_inc(S.v1, 1)
    V.wait_ge(S.p1, 2)
    V.wait_ge(S.v1, 1)
    V.tensor_tensor(T.msk[:], T.ps_s[:, 0:2 * N], T.pen[:], AluOpType.min).then_inc(S.v2, 1)
    V.wait_ge(S.v2, 1)
    for h in range(2):
        V.tensor_reduce(T.negm[:, h:h + 1], T.msk[:, h * N:(h + 1) * N], AxisListType.X, AluOpType.max,
                        negate=True).then_inc(S.v3, 1)
    A.wait_ge(S.v3, 2)
    for h in range(2):
        A.activation(T.ex[:, h * N:(h + 1) * N], T.msk[:, h * N:(h + 1) * N], ActivationFunctionType.Exp,
                     bias=T.negm[:, h:h + 1], scale=1.0, accum_out=T.ssum[:, h:h + 1]).then_inc(S.a_e, 1)
    V.wait_ge(S.c2, 1)
    V.wait_ge(S.a_z, 1)
    made = [e for e in range(N) if e not in got_e]
    for e in made:
        V.tensor_scalar(T.sel[0:N, e * D:(e + 1) * D], T.one2[0:N, 0:D], T.ident[0:N, e:e + 1], None,
                        AluOpType.mult).then_inc(S.c3, 1)
    V.wait_ge(S.a_e, 2)
    V.reciprocal(T.rs[:], T.ssum[:]).then_inc(S.v4, 1)
    V.wait_ge(S.v4, 1)
    for h in range(2):
        V.tensor_scalar(T.gt[:, h * N:(h + 1) * N], T.ex[:, h * N:(h + 1) * N], T.rs[:, h:h + 1], None,
                        AluOpType.mult).then_inc(S.v5, 1)

    P.wait_ge(S.v5, 2)
    for h in range(2):
        P.matmul(T.ps_g[0:N, h * 128:(h + 1) * 128], T.gt[:, h * N:(h + 1) * N], T.ident[:], True, True).then_inc(S.p3, 1)
    V.wait_ge(S.p3, 2)
    V.tensor_copy(T.g10[0:N, :], T.ps_g[0:N, 0:TOK]).then_inc(S.v6, 1)
    P.wait_ge(S.v6, 1)
    P.wait_ge(S.c3, len(made))
    V.wait_ge(S.ld_x, 16)
    waited = False
    for i, e in enumerate(order):
        bank = T["ps_b%d" % (i % NB)]
        if i >= NB:
            P.wait_ge(S["vx%d" % order[i - NB]], 1)
        if e in got_e and not waited:
            P.wait_ge(S.sl, got_n)
            waited = True
        P.matmul(bank[:, 0:TOK], T.sel[0:N, e * D:(e + 1) * D], T.g10[0:N, :], True, True).then_inc(S["pb%d" % e], 1)
        V.wait_ge(S["pb%d" % e], 1)
        V.tensor_tensor(T.xg[:, e * TOK:(e + 1) * TOK], bank[:, 0:TOK], T.xs[:], AluOpType.mult).then_inc(S["vx%d" % e], 1)

    for i, e in enumerate(order):
        P.wait_ge(S["vx%d" % e], 1)
        if e == rank:
            P.wait_ge(S.ld_w, 16)
        else:
            P.wait_ge(S["a%d" % e], when[e][1])
        mm = P.matmul(T.ps_y[:, 0:TOK], T.wall[:, e * D:(e + 1) * D], T.xg[:, e * TOK:(e + 1) * TOK], i == 0, i == N - 1)
        if i == N - 1:
            mm.then_inc(S.py, 1)
    V.wait_ge(S.py, 1)
    V.tensor_copy(T.ys[:], T.ps_y[:, 0:TOK]).then_inc(S.v7, 1)
    g.sync.wait_ge(S.v7, 1)
    g.sync.dma_start(T.y[:], T.ys[:]).then_inc(S.st, 16)
    g.sync.wait_ge(S.st, 16)
    g.wait_ge(S.sent, sent)
